import numpy as np
import ml_dtypes


def mxq(x, axis, fmt="e4m3"):
    dtype, down = {"e4m3": (ml_dtypes.float8_e4m3fn, 7), "e5m2": (ml_dtypes.float8_e5m2, 14)}[fmt]
    v = np.moveaxis(np.asarray(x, np.float32).astype(ml_dtypes.bfloat16).astype(np.float64), axis, -1)
    blocks = v.reshape(v.shape[:-1] + (-1, 32))
    amax = np.abs(blocks).max(-1, keepdims=True)
    byte = np.maximum(np.where(amax > 0, np.frexp(amax)[1] - 1 + 127, 0) - down, 1)
    scale = np.exp2(byte - 127.0)
    codes = (blocks / scale).astype(np.float32).astype(dtype).astype(np.float64)
    return np.moveaxis((codes * scale).reshape(v.shape), -1, axis)


WIDE = False


def mx_kscale(k):
    if not WIDE:
        return np.ones(k)
    levels = np.array([30, -30])
    if k % 512:
        return np.exp2(np.random.permutation(np.resize(levels, k // 32))).repeat(32)
    a = np.empty((k // 512, 16))
    for p in range(k // 512):
        a[p, :8] = np.random.permutation(np.resize(levels, 8))
        for g in range(8):
            far = levels[np.abs(levels - a[p, g]) >= 10]
            a[p, g + 8] = far[np.random.randint(len(far))]
    return np.exp2(a.ravel()).repeat(32)


def f64(x):
    return np.asarray(x).astype(np.float64)


def striped(idx):
    return np.tile(np.asarray(idx).reshape(-1, 16).T, (8, 1)).astype(np.uint16)


def unstriped(offs):
    return offs[:16].T.reshape(-1).astype(np.int64)


E2M1 = np.array([0.0, 0.5, 1.0, 1.5, 2.0, 3.0, 4.0, 6.0, -0.0, -0.5, -1.0, -1.5, -2.0, -3.0, -4.0, -6.0])


def pack_weight(w, fmt):
    k, n = w.shape
    w = f64(np.asarray(w, np.float32).astype(ml_dtypes.bfloat16)).reshape(k // 32, 32, n)
    amax = np.abs(w).max(1)
    if fmt == "e4m3":
        byte = np.frexp(amax)[1] - 1 + 127 - 7
    else:
        mant, ex = np.frexp(amax / 6.0)
        byte = np.where(mant > 0.5, ex, ex - 1) + 127
    byte = np.clip(np.where(amax > 0, byte, 1), 1, 254)
    scaled = (w * np.exp2(127.0 - byte)[:, None, :]).reshape(k, n).astype(np.float32)
    by_word = np.ascontiguousarray(scaled.reshape(k // 512, 128, 4, n).transpose(0, 1, 3, 2))
    if fmt == "e4m3":
        words = by_word.astype(ml_dtypes.float8_e4m3fn).view(np.uint8)
    else:
        c = by_word.astype(ml_dtypes.float4_e2m1fn).view(np.uint8) & 0xF
        words = (c[..., 0::2] | (c[..., 1::2] << 4)).reshape(k // 512, 128, 2 * n)
    return np.ascontiguousarray(words), np.ascontiguousarray(byte.astype(np.uint8).reshape(k // 512, 16, n))


def unpack_weight(words, scales, fmt):
    g, _, n = scales.shape
    words = np.ascontiguousarray(words).reshape(g, 128, n, -1)
    if fmt == "e4m3":
        vals = words.view(ml_dtypes.float8_e4m3fn).astype(np.float64)
    else:
        nib = np.empty((g, 128, n, 4), np.uint8)
        nib[..., 0::2] = words & 0xF
        nib[..., 1::2] = words >> 4
        vals = E2M1[nib]
    vals = vals * np.repeat(np.exp2(scales.astype(np.float64) - 127.0), 8, axis=1)[..., None]
    return vals.transpose(0, 1, 3, 2).reshape(g * 512, n)


K, T, J, R, O, N, L, E = 512, 2048, 256, 512, 128, 256, 512, 1024


def setup_inputs():
    n = np.random.standard_normal
    idx = np.random.permutation(T)[:J]
    idx2 = np.random.permutation(T)[:J]
    idx3 = np.random.permutation(J)[:O]
    idx4 = np.random.permutation(J)[:O]
    idx5 = np.random.permutation(E)[:O]
    fk = mx_kscale(K)
    fr = mx_kscale(R)
    fl = mx_kscale(L)
    xtp = pack_weight(n((K, T)) / fk[:, None], "e2m1")
    wp = pack_weight(n((K, R)) * 1 / np.sqrt(K) * fk[:, None] * fr, "e4m3")
    wbp = pack_weight(n((R, N)) * 1 / np.sqrt(R) / fr[:, None], "e2m1")
    sxp = pack_weight(n((L, O)) / fl[:, None], "e4m3")
    wsp = pack_weight(n((L, N)) * 1 / np.sqrt(L) * fl[:, None], "e4m3")
    return {
        "xt_words": xtp[0],
        "xt_scales": xtp[1],
        "w_words": wp[0],
        "w_scales": wp[1],
        "wb_words": wbp[0],
        "wb_scales": wbp[1],
        "sx_words": sxp[0],
        "sx_scales": sxp[1],
        "ws_words": wsp[0],
        "ws_scales": wsp[1],
        "tz": (n((N, E))).astype(np.float32),
        "offs": striped(idx),
        "offs2": striped(idx2),
        "offs3": striped(idx3),
        "offs4": striped(idx4),
        "offs5": striped(idx5),
    }


def reference(xt_words, xt_scales, w_words, w_scales, wb_words, wb_scales, sx_words, sx_scales, ws_words, ws_scales, tz, offs, offs2, offs3, offs4, offs5):
    idx = unstriped(offs)
    idx2 = unstriped(offs2)
    idx3 = unstriped(offs3)
    idx4 = unstriped(offs4)
    idx5 = unstriped(offs5)
    xtu = unpack_weight(xt_words, xt_scales, "e2m1")
    wu = unpack_weight(w_words, w_scales, "e4m3")
    wbu = unpack_weight(wb_words, wb_scales, "e2m1")
    sxu = unpack_weight(sx_words, sx_scales, "e4m3")
    wsu = unpack_weight(ws_words, ws_scales, "e4m3")
    xtidxg = xtu[:, idx]
    a = wu.T @ xtidxg
    xtidx2g = xtu[:, idx2]
    b = wu.T @ xtidx2g
    hid = np.abs(a[:, idx3] - b[:, idx4])
    hidq = mxq(hid, 0, "e5m2")
    p = wbu.T @ hidq + wsu.T @ sxu
    y = p + f64(tz)[:, idx5]
    return y

@@ -1,0 +1,149 @@
+from contextlib import ExitStack
+
+import concourse.mybir as mybir
+
+K, T, J, R, O, N, L, E = 512, 2048, 256, 512, 128, 256, 512, 1024
+FLOPS = 2 * (2 * K * R * J + R * N * O + L * N * O)
+
+F32 = mybir.dt.float32
+BF16 = mybir.dt.bfloat16
+I32 = mybir.dt.int32
+U32 = mybir.dt.uint32
+U16 = mybir.dt.uint16
+U8 = mybir.dt.uint8
+E4M3X4 = mybir.dt.float8_e4m3fn_x4
+E5M2X4 = mybir.dt.float8_e5m2_x4
+E2M1X4 = mybir.dt.float4_e2m1fn_x4
+ALU = mybir.AluOpType
+ACT = mybir.ActivationFunctionType
+
+P = 128
+PACK = 4
+QUADS = 4
+
+
+def tile_list_tied_looked_skip_tabled_kernel(
+    tc, xt_words, xt_scales, w_words, w_scales, wb_words, wb_scales, sx_words, sx_scales,
+    ws_words, ws_scales, tz, offs, offs2, offs3, offs4, offs5, out,
+):
+    nc = tc.nc
+    with ExitStack() as ctx:
+        lists = ctx.enter_context(tc.tile_pool(name="lists", bufs=1))
+        sb = ctx.enter_context(tc.tile_pool(name="sb", bufs=1))
+        psum = ctx.enter_context(tc.psum_pool(name="psum", bufs=1))
+
+        def load_list(src, name):
+            tile = lists.tile(list(src.shape), U16, name=name)
+            nc.sync.dma_start(tile[:], src)
+            return tile
+
+        def load_bytes(queue, src, dtype, width, name):
+            tile = sb.tile([P, width], dtype, name=name, align_bytes=64)
+            queue.dma_start(tile[:].bitcast(I32), src.bitcast(I32))
+            return tile
+
+        def load_plane_quads(queue, src, name):
+            width = src.shape[2]
+            tile = sb.tile([P, width], U8, name=name, align_bytes=64)
+            nc.vector.memset(tile[:].bitcast(I32), 0)
+            for q in range(QUADS):
+                queue.dma_start(tile[32 * q : 32 * q + 4, :].bitcast(I32), src[0, 4 * q : 4 * q + 4, :].bitcast(I32))
+            return tile
+
+        list1 = load_list(offs, "list1")
+        xt_table = load_bytes(nc.sync, xt_words[0], U16, T, "xt_table")
+        xt_plane = load_plane_quads(nc.sync, xt_scales, "xt_plane")
+        w_raw = load_bytes(nc.sync, w_words[0].rearrange("p n t -> p (n t)"), U32, R, "w_raw")
+        list2 = load_list(offs2, "list2")
+        w_plane = load_plane_quads(nc.scalar, w_scales, "w_plane")
+        list3 = load_list(offs3, "list3")
+        list4 = load_list(offs4, "list4")
+        list5 = load_list(offs5, "list5")
+        tz_rows = sb.tile([P, N // P, E], F32)
+        nc.sync.dma_start(tz_rows[:], tz.rearrange("(h p) e -> p h e", p=P))
+        sx_codes = load_bytes(nc.sync, sx_words[0].rearrange("p n t -> p (n t)"), U32, O, "sx_codes")
+        ws_codes = load_bytes(nc.sync, ws_words[0].rearrange("p n t -> p (n t)"), U32, N, "ws_codes")
+        wb_codes = load_bytes(nc.sync, wb_words[0], U16, N, "wb_codes")
+        sx_plane = load_plane_quads(nc.gpsimd, sx_scales, "sx_plane")
+        ws_plane = load_plane_quads(nc.sync, ws_scales, "ws_plane")
+        wb_plane = load_plane_quads(nc.sync, wb_scales, "wb_plane")
+
+        def gather_tokens(offsets, name):
+            words = sb.tile([P, J], U16, name=name + "_words", align_bytes=64)
+            plane = sb.tile([P, J], U8, name=name + "_plane", align_bytes=64)
+            nc.vector.tensor_copy(plane[:], xt_plane[:].indirect(offsets[:]))
+            nc.vector.tensor_copy(words[:], xt_table[:].indirect(offsets[:]))
+            return words, plane
+
+        w_dealt = sb.tile([P, PACK, P], U32, align_bytes=64)
+        w_plane_dealt = sb.tile([P, PACK, P], U8, align_bytes=64)
+        nc.scalar.copy(w_dealt[:].rearrange("p t m -> p m t"), w_raw[:].rearrange("p (m t) -> p m t", t=PACK))
+        nc.vector.tensor_copy(
+            w_plane_dealt[:].rearrange("p t m -> p m t"), w_plane[:].rearrange("p (m t) -> p m t", t=PACK)
+        )
+
+        def first_product(words, plane, name):
+            banks = []
+            for t in range(PACK):
+                bank = psum.tile([P, J], F32, name=name + str(t))
+                nc.tensor.matmul_mx(
+                    out=bank[:], lhsT=w_dealt[:, t, :].bitcast(E4M3X4), lhsT_scale=w_plane_dealt[:, t, :],
+                    rhs=words[:].bitcast(E2M1X4), rhs_scale=plane[:], start=True, stop=True,
+                )
+                banks.append(bank)
+            return banks
+
+        xa_words, xa_plane = gather_tokens(list1, "xa")
+        a_banks = first_product(xa_words, xa_plane, "bank_a")
+        xb_words, xb_plane = gather_tokens(list2, "xb")
+        b_banks = first_product(xb_words, xb_plane, "bank_b")
+
+        a_rows = [sb.tile([P, J], F32, name="a_rows" + str(t)) for t in range(PACK)]
+        b_rows = [sb.tile([P, J], F32, name="b_rows" + str(t)) for t in range(PACK)]
+        a_picked = [sb.tile([P, O], F32, name="a_picked" + str(t)) for t in range(PACK)]
+        diff = sb.tile([P, PACK, O], F32)
+
+        for t in range(PACK):
+            nc.scalar.copy(a_rows[t][:], a_banks[t][:])
+        for t in range(PACK):
+            nc.scalar.activation(a_picked[t][:], a_rows[t][:].indirect(list3[:]), ACT.Copy)
+            if t < 2:
+                nc.vector.tensor_copy(b_rows[t][:], b_banks[t][:])
+            else:
+                nc.scalar.copy(b_rows[t][:], b_banks[t][:])
+            nc.vector.tensor_tensor(diff[:, t, :], b_rows[t][:].indirect(list4[:]), a_picked[t][:], ALU.subtract)
+
+        hid = sb.tile([P, O, PACK], BF16, align_bytes=64)
+        diff_by_place = diff[:].rearrange("p t o -> p o t")
+        half = O // 2
+        nc.scalar.activation(hid[:, :half, :], diff_by_place[:, :half, :], ACT.Abs)
+        nc.vector.scalar_tensor_tensor(
+            hid[:, half:, :], diff_by_place[:, half:, :], -1.0, diff_by_place[:, half:, :], ALU.mult, ALU.max
+        )
+        hid_words = sb.tile([P, O], U32, align_bytes=64)
+        hid_plane = sb.tile([P, O], U8, align_bytes=64)
+        nc.vector.quantize_mx(
+            out=hid_words[:].bitcast(E5M2X4), scales=hid_plane[:], in_=hid[:].rearrange("p o t -> p (o t)")
+        )
+
+        out_banks = []
+        for h in range(N // P):
+            bank = psum.tile([P, J], F32, name="out_bank" + str(h), tag="bank_b" + str(2 + h))
+            nc.tensor.matmul_mx(
+                out=bank[:, :O], lhsT=ws_codes[:, h * P : (h + 1) * P].bitcast(E4M3X4),
+                lhsT_scale=ws_plane[:, h * P : (h + 1) * P],
+                rhs=sx_codes[:].bitcast(E4M3X4), rhs_scale=sx_plane[:], start=True, stop=False,
+            )
+            out_banks.append(bank)
+        for h, bank in enumerate(out_banks):
+            nc.tensor.matmul_mx(
+                out=bank[:, :O], lhsT=wb_codes[:, h * P : (h + 1) * P].bitcast(E2M1X4),
+                lhsT_scale=wb_plane[:, h * P : (h + 1) * P],
+                rhs=hid_words[:].bitcast(E5M2X4), rhs_scale=hid_plane[:], start=False, stop=True,
+            )
+        for h, bank in enumerate(out_banks):
+            tz_picked = sb.tile([P, O], F32, name="tz_picked" + str(h), tag="a_picked" + str(2 + h))
+            nc.scalar.activation(tz_picked[:], tz_rows[:, h, :].indirect(list5[:]), ACT.Copy)
+            result = sb.tile([P, O], F32, name="result" + str(h))
+            nc.vector.tensor_tensor(result[:], bank[:, :O], tz_picked[:], ALU.add)
+            (nc.sync, nc.scalar)[h].dma_start(out[h * P : (h + 1) * P, :], result[:])

@@ -42,45 +42,65 @@ def tile_list_tied_looked_skip_tabled_kernel(
             queue.dma_start(tile[:].bitcast(I32), src.bitcast(I32))
             return tile
 
-        def load_plane_quads(queue, src, name):
-            width = src.shape[2]
-            tile = sb.tile([P, width], U8, name=name, align_bytes=64)
-            nc.vector.memset(tile[:].bitcast(I32), 0)
-            for q in range(QUADS):
-                queue.dma_start(tile[32 * q : 32 * q + 4, :].bitcast(I32), src[0, 4 * q : 4 * q + 4, :].bitcast(I32))
+        def zeroed_plane(engine, src, name):
+            tile = sb.tile([P, src.shape[2]], U8, name=name, align_bytes=64)
+            engine.memset(tile[:].bitcast(I32), 0)
             return tile
 
+        def load_plane_repeated(queue, tile, src, quadrants):
+            for q in quadrants:
+                rows = src[0, 4 * q : 4 * q + 4, :].bitcast(I32).unsqueeze(0).to_broadcast([8, 4, src.shape[2] // 4])
+                queue.dma_start(tile[32 * q : 32 * q + 32, :].bitcast(I32), rows)
+
+        def load_plane_rows(queue, tile, src, quadrants):
+            for q in quadrants:
+                queue.dma_start(tile[32 * q : 32 * q + 4, :].bitcast(I32), src[0, 4 * q : 4 * q + 4, :].bitcast(I32))
+
+        w_plane = zeroed_plane(nc.vector, w_scales, "w_plane")
+        ws_plane = zeroed_plane(nc.vector, ws_scales, "ws_plane")
+        wb_plane = zeroed_plane(nc.vector, wb_scales, "wb_plane")
+        xt_plane = sb.tile([P, T], U8, align_bytes=64)
+        sx_plane = sb.tile([P, O], U8, align_bytes=64)
         list1 = load_list(offs, "list1")
-        xt_table = load_bytes(nc.sync, xt_words[0], U16, T, "xt_table")
-        xt_plane = load_plane_quads(nc.sync, xt_scales, "xt_plane")
-        w_raw = load_bytes(nc.sync, w_words[0].rearrange("p n t -> p (n t)"), U32, R, "w_raw")
+        load_plane_repeated(nc.sync, xt_plane, xt_scales, range(QUADS))
         list2 = load_list(offs2, "list2")
-        w_plane = load_plane_quads(nc.scalar, w_scales, "w_plane")
+        xt_table = load_bytes(nc.sync, xt_words[0], U16, T, "xt_table")
+        w_raw = load_bytes(nc.sync, w_words[0].rearrange("p n t -> p (n t)"), U32, R, "w_raw")
+        load_plane_rows(nc.sync, w_plane, w_scales, range(QUADS))
         list3 = load_list(offs3, "list3")
         list4 = load_list(offs4, "list4")
-        list5 = load_list(offs5, "list5")
+        load_plane_repeated(nc.gpsimd, sx_plane, sx_scales, (0, 1))
         tz_rows = sb.tile([P, N // P, E], F32)
-        nc.sync.dma_start(tz_rows[:], tz.rearrange("(h p) e -> p h e", p=P))
-        sx_codes = load_bytes(nc.sync, sx_words[0].rearrange("p n t -> p (n t)"), U32, O, "sx_codes")
+        nc.gpsimd.dma_start(tz_rows[:], tz.rearrange("(h p) e -> p h e", p=P))
         ws_codes = load_bytes(nc.sync, ws_words[0].rearrange("p n t -> p (n t)"), U32, N, "ws_codes")
+        sx_codes = load_bytes(nc.sync, sx_words[0].rearrange("p n t -> p (n t)"), U32, O, "sx_codes")
+        load_plane_repeated(nc.sync, sx_plane, sx_scales, (2, 3))
+        load_plane_rows(nc.sync, ws_plane, ws_scales, range(QUADS))
         wb_codes = load_bytes(nc.sync, wb_words[0], U16, N, "wb_codes")
-        sx_plane = load_plane_quads(nc.gpsimd, sx_scales, "sx_plane")
-        ws_plane = load_plane_quads(nc.sync, ws_scales, "ws_plane")
-        wb_plane = load_plane_quads(nc.sync, wb_scales, "wb_plane")
+        list5 = load_list(offs5, "list5")
+        load_plane_rows(nc.sync, wb_plane, wb_scales, (0, 1, 2))
+        load_plane_rows(nc.gpsimd, wb_plane, wb_scales, (3,))
 
-        def gather_tokens(offsets, name):
-            words = sb.tile([P, J], U16, name=name + "_words", align_bytes=64)
-            plane = sb.tile([P, J], U8, name=name + "_plane", align_bytes=64)
+        def gather_plane(offsets, name):
+            plane = sb.tile([P, J], U8, name=name, align_bytes=64)
             nc.vector.tensor_copy(plane[:], xt_plane[:].indirect(offsets[:]))
+            return plane
+
+        def gather_words(offsets, name, tag):
+            words = sb.tile([P, J], U16, name=name, tag=tag, align_bytes=64)
             nc.vector.tensor_copy(words[:], xt_table[:].indirect(offsets[:]))
-            return words, plane
+            return words
+
+        xa_plane = gather_plane(list1, "xa_plane")
+        xb_plane = gather_plane(list2, "xb_plane")
+        xa_words = gather_words(list1, "xa_words", "xa_words")
 
         w_dealt = sb.tile([P, PACK, P], U32, align_bytes=64)
         w_plane_dealt = sb.tile([P, PACK, P], U8, align_bytes=64)
-        nc.scalar.copy(w_dealt[:].rearrange("p t m -> p m t"), w_raw[:].rearrange("p (m t) -> p m t", t=PACK))
-        nc.vector.tensor_copy(
-            w_plane_dealt[:].rearrange("p t m -> p m t"), w_plane[:].rearrange("p (m t) -> p m t", t=PACK)
-        )
+        for dealt, raw, copy in ((w_dealt, w_raw, nc.scalar.copy), (w_plane_dealt, w_plane, nc.vector.tensor_copy)):
+            by_slice = raw[:].rearrange("p (m t) -> p m t", t=PACK)
+            copy(dealt[:, 0, :], by_slice[:, :, 0])
+            copy(dealt[:, 1:, :].rearrange("p t m -> p m t"), by_slice[:, :, 1:])
 
         def first_product(words, plane, name):
             banks = []
@@ -93,9 +113,8 @@ def tile_list_tied_looked_skip_tabled_kernel(
                 banks.append(bank)
             return banks
 
-        xa_words, xa_plane = gather_tokens(list1, "xa")
         a_banks = first_product(xa_words, xa_plane, "bank_a")
-        xb_words, xb_plane = gather_tokens(list2, "xb")
+        xb_words = gather_words(list2, "xb_words", "w_plane")
         b_banks = first_product(xb_words, xb_plane, "bank_b")
 
         a_rows = [sb.tile([P, J], F32, name="a_rows" + str(t)) for t in range(PACK)]
@@ -105,12 +124,15 @@ def tile_list_tied_looked_skip_tabled_kernel(
 
         for t in range(PACK):
             nc.scalar.copy(a_rows[t][:], a_banks[t][:])
+        for t in range(2):
+            nc.vector.tensor_copy(a_picked[t][:], a_rows[t][:].indirect(list3[:]))
         for t in range(PACK):
-            nc.scalar.activation(a_picked[t][:], a_rows[t][:].indirect(list3[:]), ACT.Copy)
-            if t < 2:
+            if t == 0:
                 nc.vector.tensor_copy(b_rows[t][:], b_banks[t][:])
             else:
                 nc.scalar.copy(b_rows[t][:], b_banks[t][:])
+            if t >= 2:
+                nc.scalar.activation(a_picked[t][:], a_rows[t][:].indirect(list3[:]), ACT.Copy)
             nc.vector.tensor_tensor(diff[:, t, :], b_rows[t][:].indirect(list4[:]), a_picked[t][:], ALU.subtract)
 
         hid = sb.tile([P, O, PACK], BF16, align_bytes=64)

@@ -66,20 +66,19 @@ def tile_list_tied_looked_skip_tabled_kernel(
         list2 = load_list(offs2, "list2")
         xt_table = load_bytes(nc.sync, xt_words[0], U16, T, "xt_table")
         w_raw = load_bytes(nc.sync, w_words[0].rearrange("p n t -> p (n t)"), U32, R, "w_raw")
+        load_plane_repeated(nc.gpsimd, sx_plane, sx_scales, range(QUADS))
         load_plane_rows(nc.sync, w_plane, w_scales, range(QUADS))
         list3 = load_list(offs3, "list3")
         list4 = load_list(offs4, "list4")
-        load_plane_repeated(nc.gpsimd, sx_plane, sx_scales, (0, 1))
-        tz_rows = sb.tile([P, N // P, E], F32)
-        nc.gpsimd.dma_start(tz_rows[:], tz.rearrange("(h p) e -> p h e", p=P))
         ws_codes = load_bytes(nc.sync, ws_words[0].rearrange("p n t -> p (n t)"), U32, N, "ws_codes")
         sx_codes = load_bytes(nc.sync, sx_words[0].rearrange("p n t -> p (n t)"), U32, O, "sx_codes")
-        load_plane_repeated(nc.sync, sx_plane, sx_scales, (2, 3))
-        load_plane_rows(nc.sync, ws_plane, ws_scales, range(QUADS))
-        wb_codes = load_bytes(nc.sync, wb_words[0], U16, N, "wb_codes")
+        load_plane_rows(nc.sync, ws_plane, ws_scales, (0, 1, 2))
+        tz_rows = sb.tile([P, N // P, E], F32)
+        nc.sync.dma_start(tz_rows[:], tz.rearrange("(h p) e -> p h e", p=P))
+        load_plane_rows(nc.sync, ws_plane, ws_scales, (3,))
         list5 = load_list(offs5, "list5")
-        load_plane_rows(nc.sync, wb_plane, wb_scales, (0, 1, 2))
-        load_plane_rows(nc.gpsimd, wb_plane, wb_scales, (3,))
+        wb_codes = load_bytes(nc.sync, wb_words[0], U16, N, "wb_codes")
+        load_plane_rows(nc.sync, wb_plane, wb_scales, range(QUADS))
 
         def gather_plane(offsets, name):
             plane = sb.tile([P, J], U8, name=name, align_bytes=64)
@@ -99,8 +98,8 @@ def tile_list_tied_looked_skip_tabled_kernel(
         w_plane_dealt = sb.tile([P, PACK, P], U8, align_bytes=64)
         for dealt, raw, copy in ((w_dealt, w_raw, nc.scalar.copy), (w_plane_dealt, w_plane, nc.vector.tensor_copy)):
             by_slice = raw[:].rearrange("p (m t) -> p m t", t=PACK)
-            copy(dealt[:, 0, :], by_slice[:, :, 0])
-            copy(dealt[:, 1:, :].rearrange("p t m -> p m t"), by_slice[:, :, 1:])
+            for pair in (slice(0, 2), slice(2, 4)):
+                copy(dealt[:, pair, :].rearrange("p t m -> p m t"), by_slice[:, :, pair])
 
         def first_product(words, plane, name):
             banks = []
@@ -137,7 +136,7 @@ def tile_list_tied_looked_skip_tabled_kernel(
 
         hid = sb.tile([P, O, PACK], BF16, align_bytes=64)
         diff_by_place = diff[:].rearrange("p t o -> p o t")
-        half = O // 2
+        half = 80
         nc.scalar.activation(hid[:, :half, :], diff_by_place[:, :half, :], ACT.Abs)
         nc.vector.scalar_tensor_tensor(
             hid[:, half:, :], diff_by_place[:, half:, :], -1.0, diff_by_place[:, half:, :], ALU.mult, ALU.max

from contextlib import ExitStack

import concourse.mybir as mybir

K, T, J, R, O, N, L, E = 512, 2048, 256, 512, 128, 256, 512, 1024
FLOPS = 2 * (2 * K * R * J + R * N * O + L * N * O)

F32 = mybir.dt.float32
BF16 = mybir.dt.bfloat16
I32 = mybir.dt.int32
U32 = mybir.dt.uint32
U16 = mybir.dt.uint16
U8 = mybir.dt.uint8
E4M3X4 = mybir.dt.float8_e4m3fn_x4
E5M2X4 = mybir.dt.float8_e5m2_x4
E2M1X4 = mybir.dt.float4_e2m1fn_x4
ALU = mybir.AluOpType
ACT = mybir.ActivationFunctionType

P = 128
PACK = 4
QUADS = 4


def tile_list_tied_looked_skip_tabled_kernel(
    tc, xt_words, xt_scales, w_words, w_scales, wb_words, wb_scales, sx_words, sx_scales,
    ws_words, ws_scales, tz, offs, offs2, offs3, offs4, offs5, out,
):
    nc = tc.nc
    with ExitStack() as ctx:
        lists = ctx.enter_context(tc.tile_pool(name="lists", bufs=1))
        sb = ctx.enter_context(tc.tile_pool(name="sb", bufs=1))
        psum = ctx.enter_context(tc.psum_pool(name="psum", bufs=1))

        def load_list(src, name):
            tile = lists.tile(list(src.shape), U16, name=name)
            nc.sync.dma_start(tile[:], src)
            return tile

        def load_bytes(queue, src, dtype, width, name):
            tile = sb.tile([P, width], dtype, name=name, align_bytes=64)
            queue.dma_start(tile[:].bitcast(I32), src.bitcast(I32))
            return tile

        def zeroed_plane(engine, src, name):
            tile = sb.tile([P, src.shape[2]], U8, name=name, align_bytes=64)
            engine.memset(tile[:].bitcast(I32), 0)
            return tile

        def load_plane_repeated(queue, tile, src, quadrants):
            for q in quadrants:
                rows = src[0, 4 * q : 4 * q + 4, :].bitcast(I32).unsqueeze(0).to_broadcast([8, 4, src.shape[2] // 4])
                queue.dma_start(tile[32 * q : 32 * q + 32, :].bitcast(I32), rows)

        def load_plane_rows(queue, tile, src, quadrants):
            for q in quadrants:
                queue.dma_start(tile[32 * q : 32 * q + 4, :].bitcast(I32), src[0, 4 * q : 4 * q + 4, :].bitcast(I32))

        w_plane = zeroed_plane(nc.vector, w_scales, "w_plane")
        ws_plane = zeroed_plane(nc.vector, ws_scales, "ws_plane")
        wb_plane = zeroed_plane(nc.vector, wb_scales, "wb_plane")
        xt_plane = sb.tile([P, T], U8, align_bytes=64)
        sx_plane = sb.tile([P, O], U8, align_bytes=64)
        list1 = load_list(offs, "list1")
        load_plane_repeated(nc.sync, xt_plane, xt_scales, range(QUADS))
        list2 = load_list(offs2, "list2")
        xt_table = load_bytes(nc.sync, xt_words[0], U16, T, "xt_table")
        w_raw = load_bytes(nc.sync, w_words[0].rearrange("p n t -> p (n t)"), U32, R, "w_raw")
        load_plane_repeated(nc.gpsimd, sx_plane, sx_scales, range(QUADS))
        load_plane_rows(nc.sync, w_plane, w_scales, range(QUADS))
        list3 = load_list(offs3, "list3")
        list4 = load_list(offs4, "list4")
        ws_codes = load_bytes(nc.sync, ws_words[0].rearrange("p n t -> p (n t)"), U32, N, "ws_codes")
        sx_codes = load_bytes(nc.sync, sx_words[0].rearrange("p n t -> p (n t)"), U32, O, "sx_codes")
        load_plane_rows(nc.sync, ws_plane, ws_scales, (0, 1, 2))
        tz_rows = sb.tile([P, N // P, E], F32)
        nc.sync.dma_start(tz_rows[:], tz.rearrange("(h p) e -> p h e", p=P))
        load_plane_rows(nc.sync, ws_plane, ws_scales, (3,))
        list5 = load_list(offs5, "list5")
        wb_codes = load_bytes(nc.sync, wb_words[0], U16, N, "wb_codes")
        load_plane_rows(nc.sync, wb_plane, wb_scales, range(QUADS))

        def gather_plane(offsets, name):
            plane = sb.tile([P, J], U8, name=name, align_bytes=64)
            nc.vector.tensor_copy(plane[:], xt_plane[:].indirect(offsets[:]))
            return plane

        def gather_words(offsets, name, tag):
            words = sb.tile([P, J], U16, name=name, tag=tag, align_bytes=64)
            nc.vector.tensor_copy(words[:], xt_table[:].indirect(offsets[:]))
            return words

        xa_plane = gather_plane(list1, "xa_plane")
        xb_plane = gather_plane(list2, "xb_plane")
        xa_words = gather_words(list1, "xa_words", "xa_words")

        w_dealt = sb.tile([P, PACK, P], U32, align_bytes=64)
        w_plane_dealt = sb.tile([P, PACK, P], U8, align_bytes=64)
        for dealt, raw, copy in ((w_dealt, w_raw, nc.scalar.copy), (w_plane_dealt, w_plane, nc.vector.tensor_copy)):
            by_slice = raw[:].rearrange("p (m t) -> p m t", t=PACK)
            for pair in (slice(0, 2), slice(2, 4)):
                copy(dealt[:, pair, :].rearrange("p t m -> p m t"), by_slice[:, :, pair])

        def first_product(words, plane, name):
            banks = []
            for t in range(PACK):
                bank = psum.tile([P, J], F32, name=name + str(t))
                nc.tensor.matmul_mx(
                    out=bank[:], lhsT=w_dealt[:, t, :].bitcast(E4M3X4), lhsT_scale=w_plane_dealt[:, t, :],
                    rhs=words[:].bitcast(E2M1X4), rhs_scale=plane[:], start=True, stop=True,
                )
                banks.append(bank)
            return banks

        a_banks = first_product(xa_words, xa_plane, "bank_a")
        xb_words = gather_words(list2, "xb_words", "w_plane")
        b_banks = first_product(xb_words, xb_plane, "bank_b")

        a_rows = [sb.tile([P, J], F32, name="a_rows" + str(t)) for t in range(PACK)]
        b_rows = [sb.tile([P, J], F32, name="b_rows" + str(t)) for t in range(PACK)]
        a_picked = [sb.tile([P, O], F32, name="a_picked" + str(t)) for t in range(PACK)]
        diff = sb.tile([P, PACK, O], F32)

        for t in range(PACK):
            nc.scalar.copy(a_rows[t][:], a_banks[t][:])
        for t in range(2):
            nc.vector.tensor_copy(a_picked[t][:], a_rows[t][:].indirect(list3[:]))
        for t in range(PACK):
            if t == 0:
                nc.vector.tensor_copy(b_rows[t][:], b_banks[t][:])
            else:
                nc.scalar.copy(b_rows[t][:], b_banks[t][:])
            if t >= 2:
                nc.scalar.activation(a_picked[t][:], a_rows[t][:].indirect(list3[:]), ACT.Copy)
            nc.vector.tensor_tensor(diff[:, t, :], b_rows[t][:].indirect(list4[:]), a_picked[t][:], ALU.subtract)

        hid = sb.tile([P, O, PACK], BF16, align_bytes=64)
        diff_by_place = diff[:].rearrange("p t o -> p o t")
        half = 80
        nc.scalar.activation(hid[:, :half, :], diff_by_place[:, :half, :], ACT.Abs)
        nc.vector.scalar_tensor_tensor(
            hid[:, half:, :], diff_by_place[:, half:, :], -1.0, diff_by_place[:, half:, :], ALU.mult, ALU.max
        )
        hid_words = sb.tile([P, O], U32, align_bytes=64)
        hid_plane = sb.tile([P, O], U8, align_bytes=64)
        nc.vector.quantize_mx(
            out=hid_words[:].bitcast(E5M2X4), scales=hid_plane[:], in_=hid[:].rearrange("p o t -> p (o t)")
        )

        out_banks = []
        for h in range(N // P):
            bank = psum.tile([P, J], F32, name="out_bank" + str(h), tag="bank_b" + str(2 + h))
            nc.tensor.matmul_mx(
                out=bank[:, :O], lhsT=ws_codes[:, h * P : (h + 1) * P].bitcast(E4M3X4),
                lhsT_scale=ws_plane[:, h * P : (h + 1) * P],
                rhs=sx_codes[:].bitcast(E4M3X4), rhs_scale=sx_plane[:], start=True, stop=False,
            )
            out_banks.append(bank)
        for h, bank in enumerate(out_banks):
            nc.tensor.matmul_mx(
                out=bank[:, :O], lhsT=wb_codes[:, h * P : (h + 1) * P].bitcast(E2M1X4),
                lhsT_scale=wb_plane[:, h * P : (h + 1) * P],
                rhs=hid_words[:].bitcast(E5M2X4), rhs_scale=hid_plane[:], start=False, stop=True,
            )
        for h, bank in enumerate(out_banks):
            tz_picked = sb.tile([P, O], F32, name="tz_picked" + str(h), tag="a_picked" + str(2 + h))
            nc.scalar.activation(tz_picked[:], tz_rows[:, h, :].indirect(list5[:]), ACT.Copy)
            result = sb.tile([P, O], F32, name="result" + str(h))
            nc.vector.tensor_tensor(result[:], bank[:, :O], tz_picked[:], ALU.add)
            (nc.sync, nc.scalar)[h].dma_start(out[h * P : (h + 1) * P, :], result[:])
